import numpy as np
import ml_dtypes


def mxq(x, axis, fmt="e4m3"):
    dtype, down = {"e4m3": (ml_dtypes.float8_e4m3fn, 7), "e5m2": (ml_dtypes.float8_e5m2, 14)}[fmt]
    v = np.moveaxis(np.asarray(x, np.float32).astype(ml_dtypes.bfloat16).astype(np.float64), axis, -1)
    blocks = v.reshape(v.shape[:-1] + (-1, 32))
    amax = np.abs(blocks).max(-1, keepdims=True)
    byte = np.maximum(np.where(amax > 0, np.frexp(amax)[1] - 1 + 127, 0) - down, 1)
    scale = np.exp2(byte - 127.0)
    codes = (blocks / scale).astype(np.float32).astype(dtype).astype(np.float64)
    return np.moveaxis((codes * scale).reshape(v.shape), -1, axis)


WIDE = False


def mx_kscale(k):
    if not WIDE:
        return np.ones(k)
    levels = np.array([10, -10, 5, -5, 0])
    if k % 512:
        return np.exp2(np.random.permutation(np.resize(levels, k // 32))).repeat(32)
    a = np.empty((k // 512, 16))
    for p in range(k // 512):
        a[p, :8] = np.random.permutation(np.resize(levels, 8))
        for g in range(8):
            far = levels[np.abs(levels - a[p, g]) >= 10]
            a[p, g + 8] = far[np.random.randint(len(far))]
    return np.exp2(a.ravel()).repeat(32)


def f64(x):
    return np.asarray(x).astype(np.float64)


def striped(idx):
    return np.tile(idx.reshape(-1, 16).T, (8, 1)).astype(np.uint16)


def unstriped(offs):
    return offs[:16].T.reshape(-1).astype(np.int64)


def pack_weight(w):
    k, n = w.shape
    w = f64(np.asarray(w, np.float32).astype(ml_dtypes.bfloat16)).reshape(k // 32, 32, n)
    amax = np.abs(w).max(1)
    byte = np.clip(np.where(amax > 0, np.frexp(amax)[1] - 1 + 127 - 7, 1), 1, 254)
    scaled = (w * np.exp2(127.0 - byte)[:, None, :]).reshape(k, n).astype(np.float32)
    words = np.ascontiguousarray(scaled.reshape(k // 512, 128, 4, n).transpose(0, 1, 3, 2)).astype(ml_dtypes.float8_e4m3fn).view(np.uint8)
    return words, np.ascontiguousarray(byte.astype(np.uint8).reshape(k // 512, 16, n))


def unpack_weight(words, scales):
    g, p, n, _ = words.shape
    vals = np.ascontiguousarray(words).view(ml_dtypes.float8_e4m3fn).astype(np.float64) * np.repeat(np.exp2(scales.astype(np.float64) - 127.0), 8, axis=1)[..., None]
    return vals.transpose(0, 1, 3, 2).reshape(g * 512, n)


def planes(y):
    n, m = y.shape
    v = y.astype(np.float32).astype(ml_dtypes.bfloat16).astype(np.float64).reshape(n // 32, 32, m)
    top = np.abs(v).max(1)
    byte = np.clip(np.where(top > 0, np.frexp(top)[1] - 1 + 127 - 7, 1), 1, 254)
    codes = (v * np.exp2(127.0 - byte)[:, None, :]).reshape(n, m).astype(np.float32).astype(ml_dtypes.float8_e4m3fn).view(np.uint8)
    words = codes.reshape(n // 512, 128, 4, m).transpose(0, 1, 3, 2)
    return np.ascontiguousarray(words), np.ascontiguousarray(byte.astype(np.uint8).reshape(n // 512, 16, m))


def relu(v):
    return np.maximum(v, 0.0)


K, T, S, W, H, N = 512, 1024, 512, 1024, 512, 512


def setup_inputs():
    n = np.random.standard_normal
    s = mx_kscale(K)[:, None]
    u = mx_kscale(H)
    packed_xT = pack_weight(n((K, T)) * s)
    packed_eT = pack_weight(n((K, W)) * s)
    packed_yT = pack_weight(n((K, W)) * s)
    return {
        "x_words": packed_xT[0],
        "x_scales": packed_xT[1],
        "e_words": packed_eT[0],
        "e_scales": packed_eT[1],
        "y_words": packed_yT[0],
        "y_scales": packed_yT[1],
        "w1": (n((K, H)) / np.sqrt(3 * K) / s * u).astype(np.float32),
        "w2": (n((K, H)) / np.sqrt(3 * K) / s * u).astype(np.float32),
        "w3": (n((K, H)) / np.sqrt(3 * K) / s * u).astype(np.float32),
        "w4": (n((H, N)) / np.sqrt(H) / u[:, None]).astype(np.float32),
        "offs": striped(np.random.permutation(T)[:S]),
        "tok": striped(np.random.permutation(W)[:S]),
        "row": striped(np.random.permutation(W)[:S]),
    }


def reference(x_words, x_scales, e_words, e_scales, y_words, y_scales, w1, w2, w3, w4, offs, tok, row):
    xq = unpack_weight(x_words, x_scales)[:, unstriped(offs)]
    e_tok = unpack_weight(e_words, e_scales)[:, unstriped(tok)]
    y_row = unpack_weight(y_words, y_scales)[:, unstriped(row)]
    h = relu(mxq(f64(w1), 0, "e4m3").T @ xq + mxq(f64(w2), 0, "e4m3").T @ e_tok + mxq(f64(w3), 0, "e4m3").T @ y_row)
    out_0 = mxq(f64(w4), 0, "e4m3").T @ mxq(h, 0, "e4m3")
    return (out_0,) + planes(out_0)

@@ -1,0 +1,223 @@
+from contextlib import ExitStack
+
+import concourse.mybir as mybir
+
+K, T, S, H, N = 512, 1024, 512, 512, 512
+FLOPS = 2 * S * (3 * K * H + H * N)
+
+F32 = mybir.dt.float32
+BF16 = mybir.dt.bfloat16
+I32 = mybir.dt.int32
+U32 = mybir.dt.uint32
+U16 = mybir.dt.uint16
+U8 = mybir.dt.uint8
+FP8X4 = mybir.dt.float8_e4m3fn_x4
+ACT = mybir.ActivationFunctionType
+
+P = 128
+PACK = 4
+CHUNK = 128
+HALF = 256
+
+
+def tile_picked_zlayout_relu_po_kernel(
+    tc, x_words, x_scales, e_words, e_scales, y_words, y_scales, w1, w2, w3, w4, offs, tok, row, out_0, out_1, out_2
+):
+    nc = tc.nc
+    with ExitStack() as ctx:
+        keep = ctx.enter_context(tc.tile_pool(name="keep", bufs=1))
+        psum = ctx.enter_context(tc.psum_pool(name="psum", bufs=1))
+
+        def tile(shape, dtype, name):
+            return keep.tile(shape, dtype, name=name, align_bytes=64)
+
+        tables = {"x": (x_words, x_scales, offs), "e": (e_words, e_scales, tok), "y": (y_words, y_scales, row)}
+        weights = {"w1": w1, "w2": w2, "w3": w3, "w4": w4}
+
+        lists = {n: tile([P, S // 16], U16, "list_" + n) for n in tables}
+        words = {n: tile([P, T], U32, "words_" + n) for n in tables}
+        scales = {n: tile([P, T], U8, "scales_" + n) for n in tables}
+        got_words = {n: tile([P, S], U32, "got_words_" + n) for n in tables}
+        got_scales = {n: tile([P, S], U8, "got_scales_" + n) for n in tables}
+        cuts = {"w1": (0, 128, 256, 512), "w2": (0, 256, 512), "w3": (0, 256, 512), "w4": (0, 256, 512)}
+        raw = {
+            (n, a): tile([P, PACK, cuts[n][a + 1] - cuts[n][a]], F32, "raw_%s_%d" % (n, a))
+            for n in weights
+            for a in range(len(cuts[n]) - 1)
+        }
+        dealt = {n: tile([P, PACK, P, PACK], BF16, "dealt_" + n) for n in weights}
+        w_codes = {n: tile([P, PACK, P], U32, "codes_" + n) for n in weights}
+        w_scales = {n: tile([P, PACK, P], U8, "wscales_" + n) for n in weights}
+
+        def load_weight(n, a):
+            src = weights[n].rearrange("(p j) c -> p j c", j=PACK)
+            nc.sync.dma_start(out=raw[n, a][:], in_=src[:, :, cuts[n][a] : cuts[n][a + 1]])
+
+        def load_words(n):
+            nc.sync.dma_start(out=words[n][:].bitcast(I32), in_=tables[n][0][0].rearrange("p c r -> p (c r)").bitcast(I32))
+
+        def load_scales(n, quadrants):
+            for q in quadrants:
+                nc.sync.dma_start(
+                    out=scales[n][32 * q : 32 * q + 4, :].bitcast(I32), in_=tables[n][1][0][4 * q : 4 * q + 4, :].bitcast(I32)
+                )
+
+        def load_list(n):
+            nc.sync.dma_start(out=lists[n][:], in_=tables[n][2])
+
+        def round_weight(n, a, on_scalar, lo=0, hi=None):
+            m0 = cuts[n][a] // PACK
+            hi = cuts[n][a + 1] // PACK - m0 if hi is None else hi
+            src = raw[n, a][:].rearrange("p j (m t) -> p m j t", t=PACK)[:, lo:hi]
+            dst = dealt[n][:].rearrange("p t m j -> p m j t")[:, m0 + lo : m0 + hi]
+            if on_scalar:
+                nc.scalar.activation(out=dst, in_=src, func=ACT.Copy)
+            else:
+                nc.vector.tensor_copy(out=dst, in_=src)
+
+        def quantize_weight(n, t0=0, t1=PACK):
+            nc.vector.quantize_mx(
+                out=w_codes[n][:, t0:t1, :].rearrange("p t m -> p (t m)").bitcast(FP8X4),
+                scales=w_scales[n][:, t0:t1, :].rearrange("p t m -> p (t m)"),
+                in_=dealt[n][:, t0:t1].rearrange("p t m j -> p (t m j)"),
+            )
+
+        def gather(dst, window, n, lo, hi):
+            nc.vector.tensor_copy(out=dst[:, lo:hi], in_=window[:].indirect(lists[n][:, lo // 16 : hi // 16]))
+
+        h_banks = [psum.tile([P, PACK, CHUNK], F32, name="h_bank%d" % c) for c in range(S // CHUNK)]
+        o_banks = [psum.tile([P, PACK, CHUNK], F32, name="o_bank%d" % c) for c in range(S // CHUNK)]
+
+        def first_layer(w, n, c, first, last):
+            cols = slice(c * CHUNK, (c + 1) * CHUNK)
+            for t in range(PACK):
+                nc.tensor.matmul_mx(
+                    out=h_banks[c][:, t, :],
+                    lhsT=w_codes[w][:, t, :].bitcast(FP8X4),
+                    lhsT_scale=w_scales[w][:, t, :],
+                    rhs=got_words[n][:, cols].bitcast(FP8X4),
+                    rhs_scale=got_scales[n][:, cols],
+                    start=first and t == 0,
+                    stop=last and t == PACK - 1,
+                )
+
+        nc.vector.memset(scales["x"][:].bitcast(I32), 0)
+        nc.gpsimd.memset(scales["e"][:].bitcast(I32), 0)
+        nc.vector.memset(scales["y"][:].bitcast(I32), 0)
+
+        load_weight("w1", 0)
+        load_list("x")
+        load_scales("x", range(4))
+        load_weight("w1", 1)
+        load_weight("w1", 2)
+        load_words("x")
+        load_list("e")
+        load_scales("e", range(4))
+        load_weight("w2", 0)
+        load_weight("w2", 1)
+        load_list("y")
+        load_scales("y", range(4))
+        load_words("e")
+        load_weight("w3", 0)
+        load_weight("w3", 1)
+        load_weight("w4", 0)
+        load_words("y")
+        load_weight("w4", 1)
+
+        round_weight("w1", 0, True)
+        gather(got_scales["x"], scales["x"], "x", 0, S)
+        round_weight("w1", 1, True)
+        round_weight("w1", 2, True, 0, 20)
+        round_weight("w1", 2, False, 20, 64)
+        quantize_weight("w1")
+        gather(got_words["x"], words["x"], "x", 0, S)
+        for c in range(S // CHUNK):
+            first_layer("w1", "x", c, True, False)
+        gather(got_scales["e"], scales["e"], "e", 0, S)
+        round_weight("w2", 0, True)
+        round_weight("w2", 1, True)
+        gather(got_scales["y"], scales["y"], "y", 0, S)
+        gather(got_words["e"], words["e"], "e", 0, S)
+        quantize_weight("w2")
+        for c in range(S // CHUNK):
+            first_layer("w2", "e", c, False, False)
+        round_weight("w3", 0, True)
+        round_weight("w3", 1, True)
+        quantize_weight("w3")
+        round_weight("w4", 0, True)
+
+        h_round = [tile([P, CHUNK, PACK], BF16, "h_round%d" % c) for c in range(S // CHUNK)]
+        h_codes = tile([P, S], U32, "h_codes")
+        h_scales = tile([P, S], U8, "h_scales")
+
+        for c in range(S // CHUNK):
+            gather(got_words["y"], words["y"], "y", c * CHUNK, (c + 1) * CHUNK)
+            first_layer("w3", "y", c, False, True)
+            nc.scalar.activation(out=h_round[c][:], in_=h_banks[c][:].rearrange("p t n -> p n t"), func=ACT.Relu)
+
+        def quantize_h(c):
+            cols = slice(c * CHUNK, (c + 1) * CHUNK)
+            nc.vector.quantize_mx(
+                out=h_codes[:, cols].bitcast(FP8X4), scales=h_scales[:, cols], in_=h_round[c][:].rearrange("p n t -> p (n t)")
+            )
+
+        result = tile([P, PACK, S], F32, "result")
+        out_rows = out_0.rearrange("(p t) j -> p t j", t=PACK)
+        o_round = [tile([P, CHUNK, PACK], BF16, "o_round%d" % c) for c in range(S // CHUNK)]
+        o_codes = tile([P, S], U32, "o_codes")
+        o_scales = tile([P, S], U8, "o_scales")
+        code_rows = out_1[0].rearrange("p c r -> p (c r)").bitcast(I32)
+
+        def second_layer(c, on_scalar):
+            cols = slice(c * CHUNK, (c + 1) * CHUNK)
+            for t in range(PACK):
+                nc.tensor.matmul_mx(
+                    out=o_banks[c][:, t, :],
+                    lhsT=w_codes["w4"][:, t, :].bitcast(FP8X4),
+                    lhsT_scale=w_scales["w4"][:, t, :],
+                    rhs=h_codes[:, cols].bitcast(FP8X4),
+                    rhs_scale=h_scales[:, cols],
+                    start=True,
+                    stop=True,
+                )
+            if on_scalar:
+                nc.scalar.copy(out=result[:, :, cols], in_=o_banks[c][:])
+            else:
+                nc.vector.tensor_copy(out=result[:, :, cols], in_=o_banks[c][:])
+            nc.sync.dma_start(out=out_rows[:, :, cols], in_=result[:, :, cols])
+
+        def round_result(c):
+            cols = slice(c * CHUNK, (c + 1) * CHUNK)
+            nc.vector.tensor_copy(
+                out=o_round[c][:].rearrange("p (c i) t -> p c t i", i=4),
+                in_=result[:, :, cols].rearrange("p t (c i) -> p c t i", i=4),
+            )
+
+        def quantize_result(c):
+            cols = slice(c * CHUNK, (c + 1) * CHUNK)
+            nc.vector.quantize_mx(
+                out=o_codes[:, cols].bitcast(FP8X4), scales=o_scales[:, cols], in_=o_round[c][:].rearrange("p n t -> p (n t)")
+            )
+
+        round_weight("w4", 1, False)
+        quantize_h(0)
+        quantize_weight("w4")
+        quantize_h(1)
+        quantize_h(2)
+        second_layer(0, False)
+        quantize_h(3)
+        for c in range(1, S // CHUNK):
+            second_layer(c, True)
+        round_result(0)
+        round_result(1)
+        quantize_result(0)
+        quantize_result(1)
+        nc.sync.dma_start(out=code_rows[:, 0:256], in_=o_codes[:, 0:256].bitcast(I32))
+        round_result(2)
+        round_result(3)
+        quantize_result(2)
+        quantize_result(3)
+        nc.sync.dma_start(out=code_rows[:, 256:512], in_=o_codes[:, 256:512].bitcast(I32))
+        for q in range(4):
+            queue = nc.scalar if q % 2 == 0 else nc.sync
+            queue.dma_start(out=out_2[0][4 * q : 4 * q + 4, :].bitcast(I32), in_=o_scales[32 * q : 32 * q + 4, :].bitcast(I32))

@@ -26,56 +26,59 @@ def tile_picked_zlayout_relu_po_kernel(
     nc = tc.nc
     with ExitStack() as ctx:
         keep = ctx.enter_context(tc.tile_pool(name="keep", bufs=1))
+        placed = ctx.enter_context(tc.tile_pool(name="placed", bufs=1))
         psum = ctx.enter_context(tc.psum_pool(name="psum", bufs=1))
 
-        def tile(shape, dtype, name):
-            return keep.tile(shape, dtype, name=name, align_bytes=64)
+        def tile(shape, dtype, name, offset=None):
+            if offset is None:
+                return keep.tile(shape, dtype, name=name, align_bytes=64)
+            return placed.tile(shape, dtype, name=name, align_bytes=64, offset=offset)
 
         tables = {"x": (x_words, x_scales, offs), "e": (e_words, e_scales, tok), "y": (y_words, y_scales, row)}
         weights = {"w1": w1, "w2": w2, "w3": w3, "w4": w4}
 
         lists = {n: tile([P, S // 16], U16, "list_" + n) for n in tables}
-        words = {n: tile([P, T], U32, "words_" + n) for n in tables}
-        scales = {n: tile([P, T], U8, "scales_" + n) for n in tables}
-        got_words = {n: tile([P, S], U32, "got_words_" + n) for n in tables}
-        got_scales = {n: tile([P, S], U8, "got_scales_" + n) for n in tables}
-        cuts = {"w1": (0, 128, 256, 512), "w2": (0, 256, 512), "w3": (0, 256, 512), "w4": (0, 256, 512)}
+        place = {"x": 0, "e": 4 * T, "y": None}
+        words = {n: tile([P, T], U32, "words_" + n, place[n]) for n in tables}
+        scales = {n: tile([P, T], U8, "scales_" + n, 8 * T if n == "y" else None) for n in tables}
+        got_words, got_scales, w_codes = {}, {}, {}
+        cuts = {"w1": (0, 512), "w2": (0, 512), "w3": (0, 256, 512), "w4": (0, 256, 512)}
         raw = {
             (n, a): tile([P, PACK, cuts[n][a + 1] - cuts[n][a]], F32, "raw_%s_%d" % (n, a))
             for n in weights
             for a in range(len(cuts[n]) - 1)
         }
         dealt = {n: tile([P, PACK, P, PACK], BF16, "dealt_" + n) for n in weights}
-        w_codes = {n: tile([P, PACK, P], U32, "codes_" + n) for n in weights}
         w_scales = {n: tile([P, PACK, P], U8, "wscales_" + n) for n in weights}
 
         def load_weight(n, a):
             src = weights[n].rearrange("(p j) c -> p j c", j=PACK)
             nc.sync.dma_start(out=raw[n, a][:], in_=src[:, :, cuts[n][a] : cuts[n][a + 1]])
 
-        def load_words(n):
-            nc.sync.dma_start(out=words[n][:].bitcast(I32), in_=tables[n][0][0].rearrange("p c r -> p (c r)").bitcast(I32))
+        def load_words(n, lo=0, hi=T):
+            src = tables[n][0][0].rearrange("p c r -> p (c r)").bitcast(I32)
+            nc.sync.dma_start(out=words[n][:, lo:hi].bitcast(I32), in_=src[:, lo:hi])
 
-        def load_scales(n, quadrants):
+        def load_scales(n, queue, quadrants=range(4)):
             for q in quadrants:
-                nc.sync.dma_start(
+                queue.dma_start(
                     out=scales[n][32 * q : 32 * q + 4, :].bitcast(I32), in_=tables[n][1][0][4 * q : 4 * q + 4, :].bitcast(I32)
                 )
 
         def load_list(n):
             nc.sync.dma_start(out=lists[n][:], in_=tables[n][2])
 
-        def round_weight(n, a, on_scalar, lo=0, hi=None):
-            m0 = cuts[n][a] // PACK
-            hi = cuts[n][a + 1] // PACK - m0 if hi is None else hi
-            src = raw[n, a][:].rearrange("p j (m t) -> p m j t", t=PACK)[:, lo:hi]
-            dst = dealt[n][:].rearrange("p t m j -> p m j t")[:, m0 + lo : m0 + hi]
+        def round_weight(n, a, on_scalar, t0=0, t1=PACK):
+            m0, m1 = cuts[n][a] // PACK, cuts[n][a + 1] // PACK
+            src = raw[n, a][:].rearrange("p j (m t) -> p m j t", t=PACK)[:, :, :, t0:t1]
+            dst = dealt[n][:, t0:t1, m0:m1, :].rearrange("p t m j -> p m j t")
             if on_scalar:
                 nc.scalar.activation(out=dst, in_=src, func=ACT.Copy)
             else:
                 nc.vector.tensor_copy(out=dst, in_=src)
 
-        def quantize_weight(n, t0=0, t1=PACK):
+        def quantize_weight(n, reuse=None, t0=0, t1=PACK):
+            w_codes[n] = tile([P, PACK, P], U32, "codes_" + n, reuse)
             nc.vector.quantize_mx(
                 out=w_codes[n][:, t0:t1, :].rearrange("p t m -> p (t m)").bitcast(FP8X4),
                 scales=w_scales[n][:, t0:t1, :].rearrange("p t m -> p (t m)"),
@@ -107,51 +110,54 @@ def tile_picked_zlayout_relu_po_kernel(
 
         load_weight("w1", 0)
         load_list("x")
-        load_scales("x", range(4))
-        load_weight("w1", 1)
-        load_weight("w1", 2)
+        load_scales("x", nc.sync)
         load_words("x")
-        load_list("e")
-        load_scales("e", range(4))
         load_weight("w2", 0)
-        load_weight("w2", 1)
-        load_list("y")
-        load_scales("y", range(4))
+        load_list("e")
+        load_scales("e", nc.sync)
         load_words("e")
         load_weight("w3", 0)
         load_weight("w3", 1)
+        load_list("y")
+        load_scales("y", nc.sync)
         load_weight("w4", 0)
         load_words("y")
         load_weight("w4", 1)
 
+        def gather_scales(n, reuse):
+            got_scales[n] = tile([P, S], U8, "got_scales_" + n, reuse)
+            gather(got_scales[n], scales[n], n, 0, S)
+
+        def gather_words(n):
+            got_words[n] = tile([P, S], U32, "got_words_" + n)
+            gather(got_words[n], words[n], n, 0, S)
+
         round_weight("w1", 0, True)
-        gather(got_scales["x"], scales["x"], "x", 0, S)
-        round_weight("w1", 1, True)
-        round_weight("w1", 2, True, 0, 20)
-        round_weight("w1", 2, False, 20, 64)
-        quantize_weight("w1")
-        gather(got_words["x"], words["x"], "x", 0, S)
+        gather_scales("x", None)
+        gather_words("x")
+        quantize_weight("w1", place["x"])
         for c in range(S // CHUNK):
             first_layer("w1", "x", c, True, False)
-        gather(got_scales["e"], scales["e"], "e", 0, S)
         round_weight("w2", 0, True)
-        round_weight("w2", 1, True)
-        gather(got_scales["y"], scales["y"], "y", 0, S)
-        gather(got_words["e"], words["e"], "e", 0, S)
-        quantize_weight("w2")
+        gather_scales("e", place["x"] + 4 * H)
+        gather_words("e")
+        quantize_weight("w2", place["e"])
         for c in range(S // CHUNK):
             first_layer("w2", "e", c, False, False)
         round_weight("w3", 0, True)
         round_weight("w3", 1, True)
-        quantize_weight("w3")
+        gather_scales("y", place["e"] + 4 * H)
+        quantize_weight("w3", 8 * T)
         round_weight("w4", 0, True)
+        got_words["y"] = tile([P, S], U32, "got_words_y")
 
         h_round = [tile([P, CHUNK, PACK], BF16, "h_round%d" % c) for c in range(S // CHUNK)]
         h_codes = tile([P, S], U32, "h_codes")
         h_scales = tile([P, S], U8, "h_scales")
 
         for c in range(S // CHUNK):
-            gather(got_words["y"], words["y"], "y", c * CHUNK, (c + 1) * CHUNK)
+            if c < 3:
+                gather(got_words["y"], words["y"], "y", c * CHUNK, (c + 1) * CHUNK if c < 2 else S)
             first_layer("w3", "y", c, False, True)
             nc.scalar.activation(out=h_round[c][:], in_=h_banks[c][:].rearrange("p t n -> p n t"), func=ACT.Relu)
 
@@ -163,12 +169,12 @@ def tile_picked_zlayout_relu_po_kernel(
 
         result = tile([P, PACK, S], F32, "result")
         out_rows = out_0.rearrange("(p t) j -> p t j", t=PACK)
-        o_round = [tile([P, CHUNK, PACK], BF16, "o_round%d" % c) for c in range(S // CHUNK)]
+        o_round = [tile([P, HALF, PACK], BF16, "o_round%d" % a) for a in range(2)]
         o_codes = tile([P, S], U32, "o_codes")
         o_scales = tile([P, S], U8, "o_scales")
         code_rows = out_1[0].rearrange("p c r -> p (c r)").bitcast(I32)
 
-        def second_layer(c, on_scalar):
+        def second_layer(c):
             cols = slice(c * CHUNK, (c + 1) * CHUNK)
             for t in range(PACK):
                 nc.tensor.matmul_mx(
@@ -180,44 +186,47 @@ def tile_picked_zlayout_relu_po_kernel(
                     start=True,
                     stop=True,
                 )
-            if on_scalar:
-                nc.scalar.copy(out=result[:, :, cols], in_=o_banks[c][:])
-            else:
-                nc.vector.tensor_copy(out=result[:, :, cols], in_=o_banks[c][:])
+
+        def store_result(c):
+            cols = slice(c * CHUNK, (c + 1) * CHUNK)
+            nc.scalar.copy(out=result[:, :, cols], in_=o_banks[c][:])
             nc.sync.dma_start(out=out_rows[:, :, cols], in_=result[:, :, cols])
 
-        def round_result(c):
-            cols = slice(c * CHUNK, (c + 1) * CHUNK)
-            nc.vector.tensor_copy(
-                out=o_round[c][:].rearrange("p (c i) t -> p c t i", i=4),
-                in_=result[:, :, cols].rearrange("p t (c i) -> p c t i", i=4),
-            )
+        def round_result(c, from_bank):
+            dst = o_round[c // 2][:, (c % 2) * CHUNK : (c % 2 + 1) * CHUNK, :]
+            if from_bank:
+                nc.vector.tensor_copy(out=dst, in_=o_banks[c][:].rearrange("p t n -> p n t"))
+            else:
+                nc.vector.tensor_copy(
+                    out=dst.rearrange("p (c i) t -> p c t i", i=4),
+                    in_=result[:, :, c * CHUNK : (c + 1) * CHUNK].rearrange("p t (c i) -> p c t i", i=4),
+                )
 
-        def quantize_result(c):
-            cols = slice(c * CHUNK, (c + 1) * CHUNK)
+        def quantize_result(a):
+            cols = slice(a * HALF, (a + 1) * HALF)
             nc.vector.quantize_mx(
-                out=o_codes[:, cols].bitcast(FP8X4), scales=o_scales[:, cols], in_=o_round[c][:].rearrange("p n t -> p (n t)")
+                out=o_codes[:, cols].bitcast(FP8X4), scales=o_scales[:, cols], in_=o_round[a][:].rearrange("p n t -> p (n t)")
             )
+            nc.sync.dma_start(out=code_rows[:, cols], in_=o_codes[:, cols].bitcast(I32))
 
         round_weight("w4", 1, False)
         quantize_h(0)
         quantize_weight("w4")
         quantize_h(1)
         quantize_h(2)
-        second_layer(0, False)
         quantize_h(3)
-        for c in range(1, S // CHUNK):
-            second_layer(c, True)
-        round_result(0)
-        round_result(1)
+        for c in range(S // CHUNK):
+            second_layer(c)
+        store_result(0)
+        store_result(1)
+        round_result(0, False)
+        round_result(1, False)
+        store_result(2)
+        round_result(3, True)
+        store_result(3)
         quantize_result(0)
+        round_result(2, False)
         quantize_result(1)
-        nc.sync.dma_start(out=code_rows[:, 0:256], in_=o_codes[:, 0:256].bitcast(I32))
-        round_result(2)
-        round_result(3)
-        quantize_result(2)
-        quantize_result(3)
-        nc.sync.dma_start(out=code_rows[:, 256:512], in_=o_codes[:, 256:512].bitcast(I32))
         for q in range(4):
             queue = nc.scalar if q % 2 == 0 else nc.sync
             queue.dma_start(out=out_2[0][4 * q : 4 * q + 4, :].bitcast(I32), in_=o_scales[32 * q : 32 * q + 4, :].bitcast(I32))

from contextlib import ExitStack

import concourse.mybir as mybir

K, T, S, H, N = 512, 1024, 512, 512, 512
FLOPS = 2 * S * (3 * K * H + H * N)

F32 = mybir.dt.float32
BF16 = mybir.dt.bfloat16
I32 = mybir.dt.int32
U32 = mybir.dt.uint32
U16 = mybir.dt.uint16
U8 = mybir.dt.uint8
FP8X4 = mybir.dt.float8_e4m3fn_x4
ACT = mybir.ActivationFunctionType

P = 128
PACK = 4
CHUNK = 128
HALF = 256


def tile_picked_zlayout_relu_po_kernel(
    tc, x_words, x_scales, e_words, e_scales, y_words, y_scales, w1, w2, w3, w4, offs, tok, row, out_0, out_1, out_2
):
    nc = tc.nc
    with ExitStack() as ctx:
        keep = ctx.enter_context(tc.tile_pool(name="keep", bufs=1))
        placed = ctx.enter_context(tc.tile_pool(name="placed", bufs=1))
        psum = ctx.enter_context(tc.psum_pool(name="psum", bufs=1))

        def tile(shape, dtype, name, offset=None):
            if offset is None:
                return keep.tile(shape, dtype, name=name, align_bytes=64)
            return placed.tile(shape, dtype, name=name, align_bytes=64, offset=offset)

        tables = {"x": (x_words, x_scales, offs), "e": (e_words, e_scales, tok), "y": (y_words, y_scales, row)}
        weights = {"w1": w1, "w2": w2, "w3": w3, "w4": w4}

        lists = {n: tile([P, S // 16], U16, "list_" + n) for n in tables}
        place = {"x": 0, "e": 4 * T, "y": None}
        words = {n: tile([P, T], U32, "words_" + n, place[n]) for n in tables}
        scales = {n: tile([P, T], U8, "scales_" + n, 8 * T if n == "y" else None) for n in tables}
        got_words, got_scales, w_codes = {}, {}, {}
        cuts = {"w1": (0, 512), "w2": (0, 512), "w3": (0, 256, 512), "w4": (0, 256, 512)}
        raw = {
            (n, a): tile([P, PACK, cuts[n][a + 1] - cuts[n][a]], F32, "raw_%s_%d" % (n, a))
            for n in weights
            for a in range(len(cuts[n]) - 1)
        }
        dealt = {n: tile([P, PACK, P, PACK], BF16, "dealt_" + n) for n in weights}
        w_scales = {n: tile([P, PACK, P], U8, "wscales_" + n) for n in weights}

        def load_weight(n, a):
            src = weights[n].rearrange("(p j) c -> p j c", j=PACK)
            nc.sync.dma_start(out=raw[n, a][:], in_=src[:, :, cuts[n][a] : cuts[n][a + 1]])

        def load_words(n, lo=0, hi=T):
            src = tables[n][0][0].rearrange("p c r -> p (c r)").bitcast(I32)
            nc.sync.dma_start(out=words[n][:, lo:hi].bitcast(I32), in_=src[:, lo:hi])

        def load_scales(n, queue, quadrants=range(4)):
            for q in quadrants:
                queue.dma_start(
                    out=scales[n][32 * q : 32 * q + 4, :].bitcast(I32), in_=tables[n][1][0][4 * q : 4 * q + 4, :].bitcast(I32)
                )

        def load_list(n):
            nc.sync.dma_start(out=lists[n][:], in_=tables[n][2])

        def round_weight(n, a, on_scalar, t0=0, t1=PACK):
            m0, m1 = cuts[n][a] // PACK, cuts[n][a + 1] // PACK
            src = raw[n, a][:].rearrange("p j (m t) -> p m j t", t=PACK)[:, :, :, t0:t1]
            dst = dealt[n][:, t0:t1, m0:m1, :].rearrange("p t m j -> p m j t")
            if on_scalar:
                nc.scalar.activation(out=dst, in_=src, func=ACT.Copy)
            else:
                nc.vector.tensor_copy(out=dst, in_=src)

        def quantize_weight(n, reuse=None, t0=0, t1=PACK):
            w_codes[n] = tile([P, PACK, P], U32, "codes_" + n, reuse)
            nc.vector.quantize_mx(
                out=w_codes[n][:, t0:t1, :].rearrange("p t m -> p (t m)").bitcast(FP8X4),
                scales=w_scales[n][:, t0:t1, :].rearrange("p t m -> p (t m)"),
                in_=dealt[n][:, t0:t1].rearrange("p t m j -> p (t m j)"),
            )

        def gather(dst, window, n, lo, hi):
            nc.vector.tensor_copy(out=dst[:, lo:hi], in_=window[:].indirect(lists[n][:, lo // 16 : hi // 16]))

        h_banks = [psum.tile([P, PACK, CHUNK], F32, name="h_bank%d" % c) for c in range(S // CHUNK)]
        o_banks = [psum.tile([P, PACK, CHUNK], F32, name="o_bank%d" % c) for c in range(S // CHUNK)]

        def first_layer(w, n, c, first, last):
            cols = slice(c * CHUNK, (c + 1) * CHUNK)
            for t in range(PACK):
                nc.tensor.matmul_mx(
                    out=h_banks[c][:, t, :],
                    lhsT=w_codes[w][:, t, :].bitcast(FP8X4),
                    lhsT_scale=w_scales[w][:, t, :],
                    rhs=got_words[n][:, cols].bitcast(FP8X4),
                    rhs_scale=got_scales[n][:, cols],
                    start=first and t == 0,
                    stop=last and t == PACK - 1,
                )

        nc.vector.memset(scales["x"][:].bitcast(I32), 0)
        nc.gpsimd.memset(scales["e"][:].bitcast(I32), 0)
        nc.vector.memset(scales["y"][:].bitcast(I32), 0)

        load_weight("w1", 0)
        load_list("x")
        load_scales("x", nc.sync)
        load_words("x")
        load_weight("w2", 0)
        load_list("e")
        load_scales("e", nc.sync)
        load_words("e")
        load_weight("w3", 0)
        load_weight("w3", 1)
        load_list("y")
        load_scales("y", nc.sync)
        load_weight("w4", 0)
        load_words("y")
        load_weight("w4", 1)

        def gather_scales(n, reuse):
            got_scales[n] = tile([P, S], U8, "got_scales_" + n, reuse)
            gather(got_scales[n], scales[n], n, 0, S)

        def gather_words(n):
            got_words[n] = tile([P, S], U32, "got_words_" + n)
            gather(got_words[n], words[n], n, 0, S)

        round_weight("w1", 0, True)
        gather_scales("x", None)
        gather_words("x")
        quantize_weight("w1", place["x"])
        for c in range(S // CHUNK):
            first_layer("w1", "x", c, True, False)
        round_weight("w2", 0, True)
        gather_scales("e", place["x"] + 4 * H)
        gather_words("e")
        quantize_weight("w2", place["e"])
        for c in range(S // CHUNK):
            first_layer("w2", "e", c, False, False)
        round_weight("w3", 0, True)
        round_weight("w3", 1, True)
        gather_scales("y", place["e"] + 4 * H)
        quantize_weight("w3", 8 * T)
        round_weight("w4", 0, True)
        got_words["y"] = tile([P, S], U32, "got_words_y")

        h_round = [tile([P, CHUNK, PACK], BF16, "h_round%d" % c) for c in range(S // CHUNK)]
        h_codes = tile([P, S], U32, "h_codes")
        h_scales = tile([P, S], U8, "h_scales")

        for c in range(S // CHUNK):
            if c < 3:
                gather(got_words["y"], words["y"], "y", c * CHUNK, (c + 1) * CHUNK if c < 2 else S)
            first_layer("w3", "y", c, False, True)
            nc.scalar.activation(out=h_round[c][:], in_=h_banks[c][:].rearrange("p t n -> p n t"), func=ACT.Relu)

        def quantize_h(c):
            cols = slice(c * CHUNK, (c + 1) * CHUNK)
            nc.vector.quantize_mx(
                out=h_codes[:, cols].bitcast(FP8X4), scales=h_scales[:, cols], in_=h_round[c][:].rearrange("p n t -> p (n t)")
            )

        result = tile([P, PACK, S], F32, "result")
        out_rows = out_0.rearrange("(p t) j -> p t j", t=PACK)
        o_round = [tile([P, HALF, PACK], BF16, "o_round%d" % a) for a in range(2)]
        o_codes = tile([P, S], U32, "o_codes")
        o_scales = tile([P, S], U8, "o_scales")
        code_rows = out_1[0].rearrange("p c r -> p (c r)").bitcast(I32)

        def second_layer(c):
            cols = slice(c * CHUNK, (c + 1) * CHUNK)
            for t in range(PACK):
                nc.tensor.matmul_mx(
                    out=o_banks[c][:, t, :],
                    lhsT=w_codes["w4"][:, t, :].bitcast(FP8X4),
                    lhsT_scale=w_scales["w4"][:, t, :],
                    rhs=h_codes[:, cols].bitcast(FP8X4),
                    rhs_scale=h_scales[:, cols],
                    start=True,
                    stop=True,
                )

        def store_result(c):
            cols = slice(c * CHUNK, (c + 1) * CHUNK)
            nc.scalar.copy(out=result[:, :, cols], in_=o_banks[c][:])
            nc.sync.dma_start(out=out_rows[:, :, cols], in_=result[:, :, cols])

        def round_result(c, from_bank):
            dst = o_round[c // 2][:, (c % 2) * CHUNK : (c % 2 + 1) * CHUNK, :]
            if from_bank:
                nc.vector.tensor_copy(out=dst, in_=o_banks[c][:].rearrange("p t n -> p n t"))
            else:
                nc.vector.tensor_copy(
                    out=dst.rearrange("p (c i) t -> p c t i", i=4),
                    in_=result[:, :, c * CHUNK : (c + 1) * CHUNK].rearrange("p t (c i) -> p c t i", i=4),
                )

        def quantize_result(a):
            cols = slice(a * HALF, (a + 1) * HALF)
            nc.vector.quantize_mx(
                out=o_codes[:, cols].bitcast(FP8X4), scales=o_scales[:, cols], in_=o_round[a][:].rearrange("p n t -> p (n t)")
            )
            nc.sync.dma_start(out=code_rows[:, cols], in_=o_codes[:, cols].bitcast(I32))

        round_weight("w4", 1, False)
        quantize_h(0)
        quantize_weight("w4")
        quantize_h(1)
        quantize_h(2)
        quantize_h(3)
        for c in range(S // CHUNK):
            second_layer(c)
        store_result(0)
        store_result(1)
        round_result(0, False)
        round_result(1, False)
        store_result(2)
        round_result(3, True)
        store_result(3)
        quantize_result(0)
        round_result(2, False)
        quantize_result(1)
        for q in range(4):
            queue = nc.scalar if q % 2 == 0 else nc.sync
            queue.dma_start(out=out_2[0][4 * q : 4 * q + 4, :].bitcast(I32), in_=o_scales[32 * q : 32 * q + 4, :].bitcast(I32))
